import numpy as np
import ml_dtypes


def mxq(x, axis, fmt="e4m3"):
    dtype, down = {"e4m3": (ml_dtypes.float8_e4m3fn, 7), "e5m2": (ml_dtypes.float8_e5m2, 14)}[fmt]
    v = np.moveaxis(np.asarray(x, np.float32).astype(ml_dtypes.bfloat16).astype(np.float64), axis, -1)
    blocks = v.reshape(v.shape[:-1] + (-1, 32))
    amax = np.abs(blocks).max(-1, keepdims=True)
    byte = np.maximum(np.where(amax > 0, np.frexp(amax)[1] - 1 + 127, 0) - down, 1)
    scale = np.exp2(byte - 127.0)
    codes = (blocks / scale).astype(np.float32).astype(dtype).astype(np.float64)
    return np.moveaxis((codes * scale).reshape(v.shape), -1, axis)


WIDE = False


def mx_kscale(k):
    if not WIDE:
        return np.ones(k)
    levels = np.array([10, -10, 5, -5, 0])
    if k % 512:
        return np.exp2(np.random.permutation(np.resize(levels, k // 32))).repeat(32)
    a = np.empty((k // 512, 16))
    for p in range(k // 512):
        a[p, :8] = np.random.permutation(np.resize(levels, 8))
        for g in range(8):
            far = levels[np.abs(levels - a[p, g]) >= 10]
            a[p, g + 8] = far[np.random.randint(len(far))]
    return np.exp2(a.ravel()).repeat(32)


def f64(x):
    return np.asarray(x).astype(np.float64)


def striped8(idx):
    return np.asarray(idx).reshape(8, -1, 16).transpose(0, 2, 1).reshape(128, -1).astype(np.uint16)


def unstriped8(offs):
    return offs.reshape(8, 16, -1).transpose(0, 2, 1).reshape(8, -1).astype(np.int64)


def pick8(x, idx, run):
    r = np.arange(len(x))
    return x[r[:, None], idx[r % (8 * run) // run]]


E2M1 = np.array([0.0, 0.5, 1.0, 1.5, 2.0, 3.0, 4.0, 6.0, -0.0, -0.5, -1.0, -1.5, -2.0, -3.0, -4.0, -6.0])


def pack_weight(w, fmt):
    k, n = w.shape
    w = f64(np.asarray(w, np.float32).astype(ml_dtypes.bfloat16)).reshape(k // 32, 32, n)
    amax = np.abs(w).max(1)
    if fmt == "e4m3":
        byte = np.frexp(amax)[1] - 1 + 127 - 7
    else:
        mant, ex = np.frexp(amax / 6.0)
        byte = np.where(mant > 0.5, ex, ex - 1) + 127
    byte = np.clip(np.where(amax > 0, byte, 1), 1, 254)
    scaled = (w * np.exp2(127.0 - byte)[:, None, :]).reshape(k, n).astype(np.float32)
    by_word = np.ascontiguousarray(scaled.reshape(k // 512, 128, 4, n).transpose(0, 1, 3, 2))
    if fmt == "e4m3":
        words = by_word.astype(ml_dtypes.float8_e4m3fn).view(np.uint8)
    else:
        c = by_word.astype(ml_dtypes.float4_e2m1fn).view(np.uint8) & 0xF
        words = (c[..., 0::2] | (c[..., 1::2] << 4)).reshape(k // 512, 128, 2 * n)
    return np.ascontiguousarray(words), np.ascontiguousarray(byte.astype(np.uint8).reshape(k // 512, 16, n))


def unpack_weight(words, scales, fmt):
    g, _, n = scales.shape
    words = np.ascontiguousarray(words).reshape(g, 128, n, -1)
    if fmt == "e4m3":
        vals = words.view(ml_dtypes.float8_e4m3fn).astype(np.float64)
    else:
        nib = np.empty((g, 128, n, 4), np.uint8)
        nib[..., 0::2] = words & 0xF
        nib[..., 1::2] = words >> 4
        vals = E2M1[nib]
    vals = vals * np.repeat(np.exp2(scales.astype(np.float64) - 127.0), 8, axis=1)[..., None]
    return vals.transpose(0, 1, 3, 2).reshape(g * 512, n)


D, T, Q, I, E = 512, 1024, 128, 512, 512


def setup_inputs():
    n = np.random.standard_normal
    idx = np.stack([np.random.permutation(T)[:I] for _ in range(8)])
    idx2 = np.stack([np.random.permutation(T)[:I] for _ in range(8)])
    fd = mx_kscale(D)
    ft = mx_kscale(T)
    keysp = pack_weight(n((D, T)) / fd[:, None], "e2m1")
    return {
        "query": (n((D, Q)) * 0.6 / np.sqrt(D) * fd[:, None]).astype(np.float32),
        "keys_words": keysp[0],
        "keys_scales": keysp[1],
        "share": (np.random.uniform(0.4, 1.0, (Q, 1))).astype(np.float32),
        "fac": (np.random.uniform(8.0, 32.0, (1, T)) * ft).astype(np.float32),
        "vals": (n((T, E)) / ft[:, None]).astype(np.float32),
        "offs": striped8(idx),
        "offs2": striped8(idx2),
    }


def reference(query, keys_words, keys_scales, share, fac, vals, offs, offs2):
    idx = unstriped8(offs)
    idx2 = unstriped8(offs2)
    keysu = unpack_weight(keys_words, keys_scales, "e2m1")
    queryq = mxq(f64(query), 0, "e4m3")
    a = queryq.T @ keysu
    dl = (pick8(a, idx2, 16) - pick8(a, idx, 16)) * f64(share)
    df = np.zeros((Q, T))
    df[np.arange(Q)[:, None], idx[np.arange(Q) % 128 // 16]] = dl
    s = a + df
    p = np.exp(s - np.max(s, axis=1, keepdims=True))
    w = p * f64(fac) / np.sum(p, axis=1, keepdims=True)
    wt = w.T
    wtq = mxq(wt, 0, "e4m3")
    valsq = mxq(f64(vals), 0, "e4m3")
    o = wtq.T @ valsq
    return o

@@ -1,0 +1,197 @@
+from contextlib import ExitStack
+
+import concourse.mybir as mybir
+from concourse.masks import make_identity
+
+D, T, Q, SLOTS, E = 512, 1024, 128, 512, 512
+FLOPS = 2 * Q * D * T + 2 * Q * T * E
+
+F32 = mybir.dt.float32
+BF16 = mybir.dt.bfloat16
+I32 = mybir.dt.int32
+U32 = mybir.dt.uint32
+U16 = mybir.dt.uint16
+U8 = mybir.dt.uint8
+FP8X4 = mybir.dt.float8_e4m3fn_x4
+FP4X4 = mybir.dt.float4_e2m1fn_x4
+ALU = mybir.AluOpType
+ACT = mybir.ActivationFunctionType
+AXIS = mybir.AxisListType
+
+P = 128
+PACK = 4
+K_PASS = P * PACK
+PASSES = T // K_PASS
+SCORE_N = 256
+OUT_N = 256
+HALF = SLOTS // 2
+LIST_COLS = HALF // 16
+
+
+def tile_attend_swapscores_heads_kernel(tc, query, keys_words, keys_scales, share, fac, vals, offs, offs2, out):
+    nc = tc.nc
+    with ExitStack() as ctx:
+        sb = ctx.enter_context(tc.tile_pool(name="sb", bufs=1))
+        ps = ctx.enter_context(tc.psum_pool(name="ps", bufs=1))
+
+        key_scale = sb.tile([P, T], U8, name="key_scale", align_bytes=64)
+        nc.vector.memset(key_scale[:].bitcast(I32), 0)
+        q_raw = sb.tile([P, PACK, Q], F32, name="q_raw", tag="stage0", align_bytes=64)
+        nc.sync.dma_start(out=q_raw[:], in_=query.rearrange("(p j) q -> p j q", j=PACK))
+        for quad in range(4):
+            nc.sync.dma_start(
+                out=key_scale[32 * quad : 32 * quad + 4, :].bitcast(I32),
+                in_=keys_scales[0, 4 * quad : 4 * quad + 4, :].bitcast(I32),
+            )
+        key_words = sb.tile([P, 2 * T], U8, name="key_words", align_bytes=64)
+        nc.sync.dma_start(out=key_words[:].bitcast(I32), in_=keys_words[0].bitcast(I32))
+        list1 = sb.tile([P, SLOTS // 16], U16, name="list1")
+        nc.sync.dma_start(list1[:], offs)
+        list2 = sb.tile([P, SLOTS // 16], U16, name="list2")
+        nc.sync.dma_start(list2[:], offs2)
+        share_col = sb.tile([P, 1], F32, name="share_col")
+        nc.gpsimd.dma_start(out=share_col[:], in_=share)
+        fac_cols = sb.tile([P, PASSES, PACK], F32, name="fac_cols")
+        nc.gpsimd.dma_start(out=fac_cols[:], in_=fac.rearrange("o (g p j) -> p (o g) j", g=PASSES, j=PACK))
+
+        moved = sb.tile([P, T], F32, name="moved")
+        nc.vector.memset(moved[:], 0.0)
+        ident = sb.tile([P, P], F32, name="ident")
+        make_identity(nc, ident[:])
+
+        share_wide = sb.tile([P, HALF], F32, name="share_wide")
+        nc.scalar.activation(share_wide[:], share_col[:].to_broadcast([P, HALF]), ACT.Copy)
+        share_neg = sb.tile([P, 1], F32, name="share_neg")
+        nc.scalar.activation(share_neg[:], share_col[:], ACT.Copy, scale=-1.0)
+
+        q_bf = sb.tile([P, Q, PACK], BF16, name="q_bf", tag="stage1", align_bytes=64)
+        nc.vector.tensor_copy(
+            out=q_bf[:].rearrange("p (c i) j -> p c j i", i=4),
+            in_=q_raw[:].rearrange("p j (c i) -> p c j i", i=4),
+        )
+        q_codes = sb.tile([P, Q], U32, name="q_codes", align_bytes=64)
+        q_scale = sb.tile([P, Q], U8, name="q_scale", align_bytes=64)
+        nc.vector.quantize_mx(out=q_codes[:].bitcast(FP8X4), scales=q_scale[:], in_=q_bf[:].rearrange("p q j -> p (q j)"))
+
+        v_raw = []
+        for g in range(PASSES):
+            raw = sb.tile([P, PACK, E], F32, name=f"v_raw{g}", tag=f"stage{g}", align_bytes=64)
+            nc.sync.dma_start(out=raw[:], in_=vals[g * K_PASS : (g + 1) * K_PASS, :].rearrange("(p j) e -> p j e", j=PACK))
+            v_raw.append(raw)
+
+        scores = sb.tile([P, T], F32, name="scores")
+        for n in range(T // SCORE_N):
+            cols = slice(n * SCORE_N, (n + 1) * SCORE_N)
+            bank = ps.tile([P, SCORE_N], F32, name=f"score_bank{n}", tag=f"bank{n}")
+            nc.tensor.matmul_mx(
+                out=bank[:],
+                lhsT=q_codes[:].bitcast(FP8X4),
+                lhsT_scale=q_scale[:],
+                rhs=key_words[:, 2 * n * SCORE_N : 2 * (n + 1) * SCORE_N].bitcast(FP4X4),
+                rhs_scale=key_scale[:, cols],
+                start=True,
+                stop=True,
+            )
+            if n % 2 == 0:
+                nc.scalar.copy(out=scores[:, cols], in_=bank[:])
+            else:
+                nc.vector.tensor_copy(out=scores[:, cols], in_=bank[:])
+
+        fac_bank = []
+        for g in range(PASSES):
+            bank = ps.tile([P, PACK, P], F32, name=f"fac_bank{g}", tag=f"bank{g}")
+            for j in range(PACK):
+                nc.tensor.transpose(bank[:, j, :], fac_cols[:, g, j : j + 1].to_broadcast([P, P]), ident[:])
+            fac_bank.append(bank)
+
+        first, second = slice(0, LIST_COLS), slice(LIST_COLS, 2 * LIST_COLS)
+        own_a = sb.tile([P, HALF], F32, name="own_a")
+        nc.vector.tensor_copy(out=own_a[:], in_=scores[:].indirect(list1[:, first]))
+        other_a = sb.tile([P, HALF], F32, name="other_a")
+        nc.scalar.activation(other_a[:], scores[:].indirect(list2[:, first]), ACT.Copy)
+        own_b = sb.tile([P, HALF], F32, name="own_b", tag="hold0", align_bytes=64)
+        nc.scalar.activation(own_b[:], scores[:].indirect(list1[:, second]), ACT.Copy)
+        other_b = sb.tile([P, HALF], F32, name="other_b", tag="hold1", align_bytes=64)
+        nc.scalar.activation(other_b[:], scores[:].indirect(list2[:, second]), ACT.Copy)
+        gap_a = sb.tile([P, HALF], F32, name="gap_a")
+        nc.vector.tensor_tensor(out=gap_a[:], in0=other_a[:], in1=own_a[:], op=ALU.subtract)
+        nc.vector.tensor_tensor(out=moved[:].indirect(list1[:, first]), in0=gap_a[:], in1=share_wide[:], op=ALU.mult)
+        own_bs = sb.tile([P, HALF], F32, name="own_bs")
+        nc.scalar.activation(own_bs[:], own_b[:], ACT.Copy, scale=share_neg[:])
+        other_bs = sb.tile([P, HALF], F32, name="other_bs")
+        nc.scalar.activation(other_bs[:], other_b[:], ACT.Copy, scale=share_col[:])
+        nc.vector.tensor_tensor(out=moved[:].indirect(list1[:, second]), in0=other_bs[:], in1=own_bs[:], op=ALU.add)
+
+        v_codes, v_scale = [], []
+        for g in range(PASSES):
+            v_bf = sb.tile([P, E, PACK], BF16, name=f"v_bf{g}", tag=f"hold{g}", align_bytes=64)
+            codes = sb.tile([P, E], U32, name=f"v_codes{g}", align_bytes=64)
+            scale = sb.tile([P, E], U8, name=f"v_scale{g}", align_bytes=64)
+            for h in range(E // OUT_N):
+                cols = slice(h * OUT_N, (h + 1) * OUT_N)
+                nc.scalar.copy(
+                    out=v_bf[:, cols, :].rearrange("p (c i) j -> p c j i", i=4),
+                    in_=v_raw[g][:, :, cols].rearrange("p j (c i) -> p c j i", i=4),
+                )
+            v_codes.append(codes)
+            v_scale.append((scale, v_bf))
+
+        s = sb.tile([P, T], F32, name="s")
+        nc.vector.tensor_tensor(out=s[:], in0=scores[:], in1=moved[:], op=ALU.add)
+        neg_max = sb.tile([P, 1], F32, name="neg_max")
+        nc.vector.tensor_reduce(out=neg_max[:], in_=s[:], axis=AXIS.X, op=ALU.max, negate=True)
+        p = sb.tile([P, T], F32, name="p", tag="stage1", align_bytes=64)
+        row_sum = sb.tile([P, 1], F32, name="row_sum")
+        nc.scalar.activation(p[:], s[:], ACT.Exp, bias=neg_max[:], accum_out=row_sum[:])
+        for g in range(PASSES):
+            scale, v_bf = v_scale[g]
+            nc.vector.quantize_mx(out=v_codes[g][:].bitcast(FP8X4), scales=scale[:], in_=v_bf[:].rearrange("p e j -> p (e j)"))
+        inv_sum = sb.tile([P, 1], F32, name="inv_sum")
+        nc.vector.reciprocal(out=inv_sum[:], in_=row_sum[:])
+
+        out_bank = [ps.tile([P, OUT_N], F32, name=f"out_bank{h}") for h in range(E // OUT_N)]
+        w_turned = []
+        for g in range(PASSES):
+            w_bf = sb.tile([P, K_PASS], BF16, name=f"w_bf{g}", align_bytes=64)
+            nc.vector.scalar_tensor_tensor(
+                out=w_bf[:].rearrange("q (p j) -> q p j", j=PACK),
+                in0=p[:, g * K_PASS : (g + 1) * K_PASS].rearrange("q (p j) -> q p j", j=PACK),
+                scalar=inv_sum[:],
+                in1=fac_bank[g][:].rearrange("q j p -> q p j"),
+                op0=ALU.mult,
+                op1=ALU.mult,
+            )
+            pairs = w_bf[:].bitcast(F32)
+            turn_bank = ps.tile([P, 2, Q], F32, name=f"turn_bank{g}")
+            for u in range(2):
+                nc.tensor.transpose(turn_bank[:, u, :], pairs[:, u : K_PASS // 2 : 2], ident[:])
+            wt_bf = sb.tile([P, Q * PACK], BF16, name=f"wt_bf{g}", align_bytes=64)
+            nc.scalar.copy(
+                out=wt_bf[:].bitcast(F32).rearrange("p (q u) -> p q u", u=2),
+                in_=turn_bank[:].rearrange("p u q -> p q u"),
+            )
+            w_turned.append(wt_bf)
+        for g in range(PASSES):
+            w_codes = sb.tile([P, Q], U32, name=f"w_codes{g}", align_bytes=64)
+            w_scale = sb.tile([P, Q], U8, name=f"w_scale{g}", align_bytes=64)
+            nc.vector.quantize_mx(out=w_codes[:].bitcast(FP8X4), scales=w_scale[:], in_=w_turned[g][:])
+            for h in range(E // OUT_N):
+                cols = slice(h * OUT_N, (h + 1) * OUT_N)
+                nc.tensor.matmul_mx(
+                    out=out_bank[h][:],
+                    lhsT=w_codes[:].bitcast(FP8X4),
+                    lhsT_scale=w_scale[:],
+                    rhs=v_codes[g][:, cols].bitcast(FP8X4),
+                    rhs_scale=v_scale[g][0][:, cols],
+                    start=(g == 0),
+                    stop=(g == PASSES - 1),
+                )
+        for h in range(E // OUT_N):
+            cols = slice(h * OUT_N, (h + 1) * OUT_N)
+            res = sb.tile([P, OUT_N], F32, name=f"res{h}")
+            if h == 0:
+                nc.vector.tensor_copy(out=res[:], in_=out_bank[h][:])
+                nc.sync.dma_start(out=out[:, cols], in_=res[:])
+            else:
+                nc.scalar.copy(out=res[:], in_=out_bank[h][:])
+                nc.scalar.dma_start(out=out[:, cols], in_=res[:])

@@ -35,7 +35,7 @@ def tile_attend_swapscores_heads_kernel(tc, query, keys_words, keys_scales, shar
         ps = ctx.enter_context(tc.psum_pool(name="ps", bufs=1))
 
         key_scale = sb.tile([P, T], U8, name="key_scale", align_bytes=64)
-        nc.vector.memset(key_scale[:].bitcast(I32), 0)
+        nc.gpsimd.memset(key_scale[:].bitcast(I32), 0)
         q_raw = sb.tile([P, PACK, Q], F32, name="q_raw", tag="stage0", align_bytes=64)
         nc.sync.dma_start(out=q_raw[:], in_=query.rearrange("(p j) q -> p j q", j=PACK))
         for quad in range(4):
@@ -43,41 +43,42 @@ def tile_attend_swapscores_heads_kernel(tc, query, keys_words, keys_scales, shar
                 out=key_scale[32 * quad : 32 * quad + 4, :].bitcast(I32),
                 in_=keys_scales[0, 4 * quad : 4 * quad + 4, :].bitcast(I32),
             )
-        key_words = sb.tile([P, 2 * T], U8, name="key_words", align_bytes=64)
+        key_words = sb.tile([P, 2 * T], U8, name="key_words", tag="stage3", align_bytes=64)
         nc.sync.dma_start(out=key_words[:].bitcast(I32), in_=keys_words[0].bitcast(I32))
         list1 = sb.tile([P, SLOTS // 16], U16, name="list1")
         nc.sync.dma_start(list1[:], offs)
         list2 = sb.tile([P, SLOTS // 16], U16, name="list2")
         nc.sync.dma_start(list2[:], offs2)
-        share_col = sb.tile([P, 1], F32, name="share_col")
-        nc.gpsimd.dma_start(out=share_col[:], in_=share)
-        fac_cols = sb.tile([P, PASSES, PACK], F32, name="fac_cols")
-        nc.gpsimd.dma_start(out=fac_cols[:], in_=fac.rearrange("o (g p j) -> p (o g) j", g=PASSES, j=PACK))
 
         moved = sb.tile([P, T], F32, name="moved")
         nc.vector.memset(moved[:], 0.0)
         ident = sb.tile([P, P], F32, name="ident")
         make_identity(nc, ident[:])
 
-        share_wide = sb.tile([P, HALF], F32, name="share_wide")
-        nc.scalar.activation(share_wide[:], share_col[:].to_broadcast([P, HALF]), ACT.Copy)
-        share_neg = sb.tile([P, 1], F32, name="share_neg")
-        nc.scalar.activation(share_neg[:], share_col[:], ACT.Copy, scale=-1.0)
 
         q_bf = sb.tile([P, Q, PACK], BF16, name="q_bf", tag="stage1", align_bytes=64)
         nc.vector.tensor_copy(
             out=q_bf[:].rearrange("p (c i) j -> p c j i", i=4),
             in_=q_raw[:].rearrange("p j (c i) -> p c j i", i=4),
         )
-        q_codes = sb.tile([P, Q], U32, name="q_codes", align_bytes=64)
-        q_scale = sb.tile([P, Q], U8, name="q_scale", align_bytes=64)
+        q_codes = sb.tile([P, Q], U32, name="q_codes", tag="stage2", align_bytes=64)
+        q_scale = sb.tile([P, Q], U8, name="q_scale", tag="stage4", align_bytes=64)
         nc.vector.quantize_mx(out=q_codes[:].bitcast(FP8X4), scales=q_scale[:], in_=q_bf[:].rearrange("p q j -> p (q j)"))
 
-        v_raw = []
-        for g in range(PASSES):
-            raw = sb.tile([P, PACK, E], F32, name=f"v_raw{g}", tag=f"stage{g}", align_bytes=64)
-            nc.sync.dma_start(out=raw[:], in_=vals[g * K_PASS : (g + 1) * K_PASS, :].rearrange("(p j) e -> p j e", j=PACK))
-            v_raw.append(raw)
+        share_col = sb.tile([P, 1], F32, name="share_col", tag="stage0", align_bytes=64)
+        nc.sync.dma_start(out=share_col[:], in_=share)
+        share_neg = sb.tile([P, 1], F32, name="share_neg")
+        nc.gpsimd.tensor_scalar(
+            out=share_neg[:], in0=share_col[:], scalar1=-1.0, scalar2=0.0, op0=ALU.mult, op1=ALU.add
+        )
+        share_wide = sb.tile([P, HALF], F32, name="share_wide")
+        nc.gpsimd.tensor_scalar(
+            out=share_wide[:], in0=share_col[:].to_broadcast([P, HALF]), scalar1=1.0, scalar2=0.0, op0=ALU.mult, op1=ALU.add
+        )
+
+        v_raw0 = sb.tile([P, PACK, E], F32, name="v_raw0", tag="stage1", align_bytes=64)
+        nc.sync.dma_start(out=v_raw0[:], in_=vals[0:K_PASS, :].rearrange("(p j) e -> p j e", j=PACK))
+        v_raw = {(0, h): v_raw0[:, :, h * OUT_N : (h + 1) * OUT_N] for h in range(2)}
 
         scores = sb.tile([P, T], F32, name="scores")
         for n in range(T // SCORE_N):
@@ -93,9 +94,18 @@ def tile_attend_swapscores_heads_kernel(tc, query, keys_words, keys_scales, shar
                 stop=True,
             )
             if n % 2 == 0:
-                nc.scalar.copy(out=scores[:, cols], in_=bank[:])
+                nc.scalar.activation(scores[:, cols], bank[:], ACT.Copy)
             else:
                 nc.vector.tensor_copy(out=scores[:, cols], in_=bank[:])
+
+        fac_cols = sb.tile([P, PASSES, PACK], F32, name="fac_cols", tag="stage4", align_bytes=64)
+        nc.sync.dma_start(out=fac_cols[:], in_=fac.rearrange("o (g p j) -> p (o g) j", g=PASSES, j=PACK))
+        for h in range(2):
+            raw = sb.tile([P, PACK, OUT_N], F32, name=f"v_raw1{h}", tag=f"stage{2 + h}", align_bytes=64)
+            nc.sync.dma_start(
+                out=raw[:], in_=vals[K_PASS:T, h * OUT_N : (h + 1) * OUT_N].rearrange("(p j) e -> p j e", j=PACK)
+            )
+            v_raw[(1, h)] = raw[:]
 
         fac_bank = []
         for g in range(PASSES):
@@ -107,7 +117,7 @@ def tile_attend_swapscores_heads_kernel(tc, query, keys_words, keys_scales, shar
         first, second = slice(0, LIST_COLS), slice(LIST_COLS, 2 * LIST_COLS)
         own_a = sb.tile([P, HALF], F32, name="own_a")
         nc.vector.tensor_copy(out=own_a[:], in_=scores[:].indirect(list1[:, first]))
-        other_a = sb.tile([P, HALF], F32, name="other_a")
+        other_a = sb.tile([P, HALF], F32, name="other_a", tag="hold2", align_bytes=64)
         nc.scalar.activation(other_a[:], scores[:].indirect(list2[:, first]), ACT.Copy)
         own_b = sb.tile([P, HALF], F32, name="own_b", tag="hold0", align_bytes=64)
         nc.scalar.activation(own_b[:], scores[:].indirect(list1[:, second]), ACT.Copy)
@@ -122,30 +132,39 @@ def tile_attend_swapscores_heads_kernel(tc, query, keys_words, keys_scales, shar
         nc.scalar.activation(other_bs[:], other_b[:], ACT.Copy, scale=share_col[:])
         nc.vector.tensor_tensor(out=moved[:].indirect(list1[:, second]), in0=other_bs[:], in1=own_bs[:], op=ALU.add)
 
-        v_codes, v_scale = [], []
-        for g in range(PASSES):
-            v_bf = sb.tile([P, E, PACK], BF16, name=f"v_bf{g}", tag=f"hold{g}", align_bytes=64)
-            codes = sb.tile([P, E], U32, name=f"v_codes{g}", align_bytes=64)
-            scale = sb.tile([P, E], U8, name=f"v_scale{g}", align_bytes=64)
-            for h in range(E // OUT_N):
-                cols = slice(h * OUT_N, (h + 1) * OUT_N)
-                nc.scalar.copy(
-                    out=v_bf[:, cols, :].rearrange("p (c i) j -> p c j i", i=4),
-                    in_=v_raw[g][:, :, cols].rearrange("p j (c i) -> p c j i", i=4),
-                )
-            v_codes.append(codes)
-            v_scale.append((scale, v_bf))
+        v_bf, v_codes, v_scale = {}, {}, {}
 
-        s = sb.tile([P, T], F32, name="s")
+        def round_values(g, h, tag):
+            v_bf[(g, h)] = sb.tile([P, OUT_N, PACK], BF16, name=f"v_bf{g}{h}", tag=tag, align_bytes=64)
+            nc.scalar.copy(
+                out=v_bf[(g, h)][:].rearrange("p (c i) j -> p c j i", i=4),
+                in_=v_raw[(g, h)].rearrange("p j (c i) -> p c j i", i=4),
+            )
+
+        def quantise_values(g, h):
+            v_codes[(g, h)] = sb.tile([P, OUT_N], U32, name=f"v_codes{g}{h}", align_bytes=64)
+            v_scale[(g, h)] = sb.tile([P, OUT_N], U8, name=f"v_scale{g}{h}", align_bytes=64)
+            nc.vector.quantize_mx(
+                out=v_codes[(g, h)][:].bitcast(FP8X4),
+                scales=v_scale[(g, h)][:],
+                in_=v_bf[(g, h)][:].rearrange("p e j -> p (e j)"),
+            )
+
+        round_values(0, 0, "hold0")
+        round_values(0, 1, "hold1")
+        round_values(1, 0, "hold2")
+
+        s = sb.tile([P, T], F32, name="s", tag="hold3", align_bytes=64)
         nc.vector.tensor_tensor(out=s[:], in0=scores[:], in1=moved[:], op=ALU.add)
         neg_max = sb.tile([P, 1], F32, name="neg_max")
         nc.vector.tensor_reduce(out=neg_max[:], in_=s[:], axis=AXIS.X, op=ALU.max, negate=True)
-        p = sb.tile([P, T], F32, name="p", tag="stage1", align_bytes=64)
+        p = sb.tile([P, T], F32, name="p", tag="stage2", align_bytes=64)
         row_sum = sb.tile([P, 1], F32, name="row_sum")
         nc.scalar.activation(p[:], s[:], ACT.Exp, bias=neg_max[:], accum_out=row_sum[:])
-        for g in range(PASSES):
-            scale, v_bf = v_scale[g]
-            nc.vector.quantize_mx(out=v_codes[g][:].bitcast(FP8X4), scales=scale[:], in_=v_bf[:].rearrange("p e j -> p (e j)"))
+        round_values(1, 1, "hold3")
+        quantise_values(0, 0)
+        quantise_values(0, 1)
+        quantise_values(1, 0)
         inv_sum = sb.tile([P, 1], F32, name="inv_sum")
         nc.vector.reciprocal(out=inv_sum[:], in_=row_sum[:])
 
@@ -171,6 +190,7 @@ def tile_attend_swapscores_heads_kernel(tc, query, keys_words, keys_scales, shar
                 in_=turn_bank[:].rearrange("p u q -> p q u"),
             )
             w_turned.append(wt_bf)
+        quantise_values(1, 1)
         for g in range(PASSES):
             w_codes = sb.tile([P, Q], U32, name=f"w_codes{g}", align_bytes=64)
             w_scale = sb.tile([P, Q], U8, name=f"w_scale{g}", align_bytes=64)
@@ -181,8 +201,8 @@ def tile_attend_swapscores_heads_kernel(tc, query, keys_words, keys_scales, shar
                     out=out_bank[h][:],
                     lhsT=w_codes[:].bitcast(FP8X4),
                     lhsT_scale=w_scale[:],
-                    rhs=v_codes[g][:, cols].bitcast(FP8X4),
-                    rhs_scale=v_scale[g][0][:, cols],
+                    rhs=v_codes[(g, h)][:].bitcast(FP8X4),
+                    rhs_scale=v_scale[(g, h)][:],
                     start=(g == 0),
                     stop=(g == PASSES - 1),
                 )

@@ -22,7 +22,7 @@ P = 128
 PACK = 4
 K_PASS = P * PACK
 PASSES = T // K_PASS
-SCORE_N = 256
+SCORE_WIDTHS = (256, 256, 256, 128, 128)
 OUT_N = 256
 HALF = SLOTS // 2
 LIST_COLS = HALF // 16
@@ -35,16 +35,17 @@ def tile_attend_swapscores_heads_kernel(tc, query, keys_words, keys_scales, shar
         ps = ctx.enter_context(tc.psum_pool(name="ps", bufs=1))
 
         key_scale = sb.tile([P, T], U8, name="key_scale", align_bytes=64)
-        nc.gpsimd.memset(key_scale[:].bitcast(I32), 0)
-        q_raw = sb.tile([P, PACK, Q], F32, name="q_raw", tag="stage0", align_bytes=64)
+        q_raw = sb.tile([P, PACK, Q], F32, name="q_raw", align_bytes=64)
         nc.sync.dma_start(out=q_raw[:], in_=query.rearrange("(p j) q -> p j q", j=PACK))
         for quad in range(4):
-            nc.sync.dma_start(
+            nc.scalar.dma_start(
                 out=key_scale[32 * quad : 32 * quad + 4, :].bitcast(I32),
                 in_=keys_scales[0, 4 * quad : 4 * quad + 4, :].bitcast(I32),
             )
-        key_words = sb.tile([P, 2 * T], U8, name="key_words", tag="stage3", align_bytes=64)
+        key_words = sb.tile([P, 2 * T], U8, name="key_words", align_bytes=64)
         nc.sync.dma_start(out=key_words[:].bitcast(I32), in_=keys_words[0].bitcast(I32))
+        share_col = sb.tile([P, 1], F32, name="share_col", tag="hold2", align_bytes=64)
+        nc.sync.dma_start(out=share_col[:], in_=share)
         list1 = sb.tile([P, SLOTS // 16], U16, name="list1")
         nc.sync.dma_start(list1[:], offs)
         list2 = sb.tile([P, SLOTS // 16], U16, name="list2")
@@ -56,56 +57,53 @@ def tile_attend_swapscores_heads_kernel(tc, query, keys_words, keys_scales, shar
         make_identity(nc, ident[:])
 
 
-        q_bf = sb.tile([P, Q, PACK], BF16, name="q_bf", tag="stage1", align_bytes=64)
+        share_wide = sb.tile([P, HALF], F32, name="share_wide")
+        nc.scalar.activation(share_wide[:], share_col[:].to_broadcast([P, HALF]), ACT.Copy)
+        share_neg = sb.tile([P, 1], F32, name="share_neg")
+        nc.scalar.activation(share_neg[:], share_col[:], ACT.Copy, scale=-1.0)
+
+        q_bf = sb.tile([P, Q, PACK], BF16, name="q_bf", align_bytes=64)
         nc.vector.tensor_copy(
             out=q_bf[:].rearrange("p (c i) j -> p c j i", i=4),
             in_=q_raw[:].rearrange("p j (c i) -> p c j i", i=4),
         )
-        q_codes = sb.tile([P, Q], U32, name="q_codes", tag="stage2", align_bytes=64)
-        q_scale = sb.tile([P, Q], U8, name="q_scale", tag="stage4", align_bytes=64)
+        q_codes = sb.tile([P, Q], U32, name="q_codes", align_bytes=64)
+        q_scale = sb.tile([P, Q], U8, name="q_scale", align_bytes=64)
         nc.vector.quantize_mx(out=q_codes[:].bitcast(FP8X4), scales=q_scale[:], in_=q_bf[:].rearrange("p q j -> p (q j)"))
 
-        share_col = sb.tile([P, 1], F32, name="share_col", tag="stage0", align_bytes=64)
-        nc.sync.dma_start(out=share_col[:], in_=share)
-        share_neg = sb.tile([P, 1], F32, name="share_neg")
-        nc.gpsimd.tensor_scalar(
-            out=share_neg[:], in0=share_col[:], scalar1=-1.0, scalar2=0.0, op0=ALU.mult, op1=ALU.add
-        )
-        share_wide = sb.tile([P, HALF], F32, name="share_wide")
-        nc.gpsimd.tensor_scalar(
-            out=share_wide[:], in0=share_col[:].to_broadcast([P, HALF]), scalar1=1.0, scalar2=0.0, op0=ALU.mult, op1=ALU.add
-        )
-
-        v_raw0 = sb.tile([P, PACK, E], F32, name="v_raw0", tag="stage1", align_bytes=64)
+        v_raw0 = sb.tile([P, PACK, E], F32, name="v_raw0", align_bytes=64)
         nc.sync.dma_start(out=v_raw0[:], in_=vals[0:K_PASS, :].rearrange("(p j) e -> p j e", j=PACK))
         v_raw = {(0, h): v_raw0[:, :, h * OUT_N : (h + 1) * OUT_N] for h in range(2)}
 
         scores = sb.tile([P, T], F32, name="scores")
-        for n in range(T // SCORE_N):
-            cols = slice(n * SCORE_N, (n + 1) * SCORE_N)
-            bank = ps.tile([P, SCORE_N], F32, name=f"score_bank{n}", tag=f"bank{n}")
+        start = 0
+        for n, width in enumerate(SCORE_WIDTHS):
+            cols = slice(start, start + width)
+            start = start + width
+            bank = ps.tile([P, width], F32, name=f"score_bank{n}", tag=f"bank{n}")
             nc.tensor.matmul_mx(
                 out=bank[:],
                 lhsT=q_codes[:].bitcast(FP8X4),
                 lhsT_scale=q_scale[:],
-                rhs=key_words[:, 2 * n * SCORE_N : 2 * (n + 1) * SCORE_N].bitcast(FP4X4),
+                rhs=key_words[:, 2 * cols.start : 2 * cols.stop].bitcast(FP4X4),
                 rhs_scale=key_scale[:, cols],
                 start=True,
                 stop=True,
             )
-            if n % 2 == 0:
+            if n in (0, 2):
                 nc.scalar.activation(scores[:, cols], bank[:], ACT.Copy)
             else:
                 nc.vector.tensor_copy(out=scores[:, cols], in_=bank[:])
 
-        fac_cols = sb.tile([P, PASSES, PACK], F32, name="fac_cols", tag="stage4", align_bytes=64)
-        nc.sync.dma_start(out=fac_cols[:], in_=fac.rearrange("o (g p j) -> p (o g) j", g=PASSES, j=PACK))
         for h in range(2):
             raw = sb.tile([P, PACK, OUT_N], F32, name=f"v_raw1{h}", tag=f"stage{2 + h}", align_bytes=64)
             nc.sync.dma_start(
                 out=raw[:], in_=vals[K_PASS:T, h * OUT_N : (h + 1) * OUT_N].rearrange("(p j) e -> p j e", j=PACK)
             )
             v_raw[(1, h)] = raw[:]
+
+        fac_cols = sb.tile([P, PASSES, PACK], F32, name="fac_cols")
+        nc.sync.dma_start(out=fac_cols[:], in_=fac.rearrange("o (g p j) -> p (o g) j", g=PASSES, j=PACK))
 
         fac_bank = []
         for g in range(PASSES):
@@ -117,7 +115,7 @@ def tile_attend_swapscores_heads_kernel(tc, query, keys_words, keys_scales, shar
         first, second = slice(0, LIST_COLS), slice(LIST_COLS, 2 * LIST_COLS)
         own_a = sb.tile([P, HALF], F32, name="own_a")
         nc.vector.tensor_copy(out=own_a[:], in_=scores[:].indirect(list1[:, first]))
-        other_a = sb.tile([P, HALF], F32, name="other_a", tag="hold2", align_bytes=64)
+        other_a = sb.tile([P, HALF], F32, name="other_a")
         nc.scalar.activation(other_a[:], scores[:].indirect(list2[:, first]), ACT.Copy)
         own_b = sb.tile([P, HALF], F32, name="own_b", tag="hold0", align_bytes=64)
         nc.scalar.activation(own_b[:], scores[:].indirect(list1[:, second]), ACT.Copy)
@@ -168,22 +166,36 @@ def tile_attend_swapscores_heads_kernel(tc, query, keys_words, keys_scales, shar
         inv_sum = sb.tile([P, 1], F32, name="inv_sum")
         nc.vector.reciprocal(out=inv_sum[:], in_=row_sum[:])
 
-        out_bank = [ps.tile([P, OUT_N], F32, name=f"out_bank{h}") for h in range(E // OUT_N)]
+        early = sb.tile([P, K_PASS // 2], F32, name="early")
+        nc.vector.tensor_tensor(
+            out=early[:].rearrange("q (p e) -> q p e", e=2),
+            in0=p[:, K_PASS:T].rearrange("q (p j) -> q p j", j=PACK)[:, :, 2:4],
+            in1=fac_bank[1][:, 2:4, :].rearrange("q e p -> q p e"),
+            op=ALU.mult,
+        )
+
+        out_parts = ((0, 0, 256), (1, 0, 128), (1, 128, 128))
+        out_bank = [
+            ps.tile([P, width], F32, name=f"out_bank{n}", tag=f"bank{2 + n}") for n, (h, first_col, width) in enumerate(out_parts)
+        ]
         w_turned = []
         for g in range(PASSES):
-            w_bf = sb.tile([P, K_PASS], BF16, name=f"w_bf{g}", align_bytes=64)
-            nc.vector.scalar_tensor_tensor(
-                out=w_bf[:].rearrange("q (p j) -> q p j", j=PACK),
-                in0=p[:, g * K_PASS : (g + 1) * K_PASS].rearrange("q (p j) -> q p j", j=PACK),
-                scalar=inv_sum[:],
-                in1=fac_bank[g][:].rearrange("q j p -> q p j"),
-                op0=ALU.mult,
-                op1=ALU.mult,
-            )
-            pairs = w_bf[:].bitcast(F32)
             turn_bank = ps.tile([P, 2, Q], F32, name=f"turn_bank{g}")
+            p_pass = p[:, g * K_PASS : (g + 1) * K_PASS].rearrange("q (p j) -> q p j", j=PACK)
             for u in range(2):
-                nc.tensor.transpose(turn_bank[:, u, :], pairs[:, u : K_PASS // 2 : 2], ident[:])
+                w_bf = sb.tile([P, K_PASS // 2], BF16, name=f"w_bf{g}{u}", align_bytes=64)
+                if (g, u) == (1, 1):
+                    nc.vector.tensor_scalar(out=w_bf[:], in0=early[:], scalar1=inv_sum[:], scalar2=None, op0=ALU.mult)
+                else:
+                    nc.vector.scalar_tensor_tensor(
+                        out=w_bf[:].rearrange("q (p e) -> q p e", e=2),
+                        in0=p_pass[:, :, 2 * u : 2 * u + 2],
+                        scalar=inv_sum[:],
+                        in1=fac_bank[g][:, 2 * u : 2 * u + 2, :].rearrange("q e p -> q p e"),
+                        op0=ALU.mult,
+                        op1=ALU.mult,
+                    )
+                nc.tensor.transpose(turn_bank[:, u, :], w_bf[:].bitcast(F32), ident[:])
             wt_bf = sb.tile([P, Q * PACK], BF16, name=f"wt_bf{g}", align_bytes=64)
             nc.scalar.copy(
                 out=wt_bf[:].bitcast(F32).rearrange("p (q u) -> p q u", u=2),
@@ -195,14 +207,14 @@ def tile_attend_swapscores_heads_kernel(tc, query, keys_words, keys_scales, shar
             w_codes = sb.tile([P, Q], U32, name=f"w_codes{g}", align_bytes=64)
             w_scale = sb.tile([P, Q], U8, name=f"w_scale{g}", align_bytes=64)
             nc.vector.quantize_mx(out=w_codes[:].bitcast(FP8X4), scales=w_scale[:], in_=w_turned[g][:])
-            for h in range(E // OUT_N):
-                cols = slice(h * OUT_N, (h + 1) * OUT_N)
+            for n, (h, first_col, width) in enumerate(out_parts):
+                cols = slice(first_col, first_col + width)
                 nc.tensor.matmul_mx(
-                    out=out_bank[h][:],
+                    out=out_bank[n][:],
                     lhsT=w_codes[:].bitcast(FP8X4),
                     lhsT_scale=w_scale[:],
-                    rhs=v_codes[(g, h)][:].bitcast(FP8X4),
-                    rhs_scale=v_scale[(g, h)][:],
+                    rhs=v_codes[(g, h)][:, cols].bitcast(FP8X4),
+                    rhs_scale=v_scale[(g, h)][:, cols],
                     start=(g == 0),
                     stop=(g == PASSES - 1),
                 )
@@ -210,8 +222,9 @@ def tile_attend_swapscores_heads_kernel(tc, query, keys_words, keys_scales, shar
             cols = slice(h * OUT_N, (h + 1) * OUT_N)
             res = sb.tile([P, OUT_N], F32, name=f"res{h}")
             if h == 0:
-                nc.vector.tensor_copy(out=res[:], in_=out_bank[h][:])
+                nc.vector.tensor_copy(out=res[:], in_=out_bank[0][:])
                 nc.sync.dma_start(out=out[:, cols], in_=res[:])
             else:
-                nc.scalar.copy(out=res[:], in_=out_bank[h][:])
+                nc.scalar.copy(out=res[:, 0:128], in_=out_bank[1][:])
+                nc.scalar.copy(out=res[:, 128:256], in_=out_bank[2][:])
                 nc.scalar.dma_start(out=out[:, cols], in_=res[:])

@@ -76,6 +76,7 @@ def tile_attend_swapscores_heads_kernel(tc, query, keys_words, keys_scales, shar
         v_raw = {(0, h): v_raw0[:, :, h * OUT_N : (h + 1) * OUT_N] for h in range(2)}
 
         scores = sb.tile([P, T], F32, name="scores")
+        score_bank = []
         start = 0
         for n, width in enumerate(SCORE_WIDTHS):
             cols = slice(start, start + width)
@@ -90,6 +91,7 @@ def tile_attend_swapscores_heads_kernel(tc, query, keys_words, keys_scales, shar
                 start=True,
                 stop=True,
             )
+            score_bank.append(bank)
             if n in (0, 2):
                 nc.scalar.activation(scores[:, cols], bank[:], ACT.Copy)
             else:
@@ -107,7 +109,7 @@ def tile_attend_swapscores_heads_kernel(tc, query, keys_words, keys_scales, shar
 
         fac_bank = []
         for g in range(PASSES):
-            bank = ps.tile([P, PACK, P], F32, name=f"fac_bank{g}", tag=f"bank{g}")
+            bank = ps.tile([P, PACK, P], F32, name=f"fac_bank{g}")
             for j in range(PACK):
                 nc.tensor.transpose(bank[:, j, :], fac_cols[:, g, j : j + 1].to_broadcast([P, P]), ident[:])
             fac_bank.append(bank)
@@ -153,7 +155,10 @@ def tile_attend_swapscores_heads_kernel(tc, query, keys_words, keys_scales, shar
         round_values(1, 0, "hold2")
 
         s = sb.tile([P, T], F32, name="s", tag="hold3", align_bytes=64)
-        nc.vector.tensor_tensor(out=s[:], in0=scores[:], in1=moved[:], op=ALU.add)
+        for n in range(3):
+            cols = slice(n * 256, (n + 1) * 256)
+            nc.vector.tensor_tensor(out=s[:, cols], in0=score_bank[n][:], in1=moved[:, cols], op=ALU.add)
+        nc.gpsimd.tensor_tensor(out=s[:, 768:T], in0=scores[:, 768:T], in1=moved[:, 768:T], op=ALU.add)
         neg_max = sb.tile([P, 1], F32, name="neg_max")
         nc.vector.tensor_reduce(out=neg_max[:], in_=s[:], axis=AXIS.X, op=ALU.max, negate=True)
         p = sb.tile([P, T], F32, name="p", tag="stage2", align_bytes=64)
@@ -180,7 +185,7 @@ def tile_attend_swapscores_heads_kernel(tc, query, keys_words, keys_scales, shar
         ]
         w_turned = []
         for g in range(PASSES):
-            turn_bank = ps.tile([P, 2, Q], F32, name=f"turn_bank{g}")
+            turn_bank = ps.tile([P, 2, Q], F32, name=f"turn_bank{g}", tag=f"bank{g}")
             p_pass = p[:, g * K_PASS : (g + 1) * K_PASS].rearrange("q (p j) -> q p j", j=PACK)
             for u in range(2):
                 w_bf = sb.tile([P, K_PASS // 2], BF16, name=f"w_bf{g}{u}", align_bytes=64)

from contextlib import ExitStack

import concourse.mybir as mybir
from concourse.masks import make_identity

D, T, Q, SLOTS, E = 512, 1024, 128, 512, 512
FLOPS = 2 * Q * D * T + 2 * Q * T * E

F32 = mybir.dt.float32
BF16 = mybir.dt.bfloat16
I32 = mybir.dt.int32
U32 = mybir.dt.uint32
U16 = mybir.dt.uint16
U8 = mybir.dt.uint8
FP8X4 = mybir.dt.float8_e4m3fn_x4
FP4X4 = mybir.dt.float4_e2m1fn_x4
ALU = mybir.AluOpType
ACT = mybir.ActivationFunctionType
AXIS = mybir.AxisListType

P = 128
PACK = 4
K_PASS = P * PACK
PASSES = T // K_PASS
SCORE_WIDTHS = (256, 256, 256, 128, 128)
OUT_N = 256
HALF = SLOTS // 2
LIST_COLS = HALF // 16


def tile_attend_swapscores_heads_kernel(tc, query, keys_words, keys_scales, share, fac, vals, offs, offs2, out):
    nc = tc.nc
    with ExitStack() as ctx:
        sb = ctx.enter_context(tc.tile_pool(name="sb", bufs=1))
        ps = ctx.enter_context(tc.psum_pool(name="ps", bufs=1))

        key_scale = sb.tile([P, T], U8, name="key_scale", align_bytes=64)
        q_raw = sb.tile([P, PACK, Q], F32, name="q_raw", align_bytes=64)
        nc.sync.dma_start(out=q_raw[:], in_=query.rearrange("(p j) q -> p j q", j=PACK))
        for quad in range(4):
            nc.scalar.dma_start(
                out=key_scale[32 * quad : 32 * quad + 4, :].bitcast(I32),
                in_=keys_scales[0, 4 * quad : 4 * quad + 4, :].bitcast(I32),
            )
        key_words = sb.tile([P, 2 * T], U8, name="key_words", align_bytes=64)
        nc.sync.dma_start(out=key_words[:].bitcast(I32), in_=keys_words[0].bitcast(I32))
        share_col = sb.tile([P, 1], F32, name="share_col", tag="hold2", align_bytes=64)
        nc.sync.dma_start(out=share_col[:], in_=share)
        list1 = sb.tile([P, SLOTS // 16], U16, name="list1")
        nc.sync.dma_start(list1[:], offs)
        list2 = sb.tile([P, SLOTS // 16], U16, name="list2")
        nc.sync.dma_start(list2[:], offs2)

        moved = sb.tile([P, T], F32, name="moved")
        nc.vector.memset(moved[:], 0.0)
        ident = sb.tile([P, P], F32, name="ident")
        make_identity(nc, ident[:])


        share_wide = sb.tile([P, HALF], F32, name="share_wide")
        nc.scalar.activation(share_wide[:], share_col[:].to_broadcast([P, HALF]), ACT.Copy)
        share_neg = sb.tile([P, 1], F32, name="share_neg")
        nc.scalar.activation(share_neg[:], share_col[:], ACT.Copy, scale=-1.0)

        q_bf = sb.tile([P, Q, PACK], BF16, name="q_bf", align_bytes=64)
        nc.vector.tensor_copy(
            out=q_bf[:].rearrange("p (c i) j -> p c j i", i=4),
            in_=q_raw[:].rearrange("p j (c i) -> p c j i", i=4),
        )
        q_codes = sb.tile([P, Q], U32, name="q_codes", align_bytes=64)
        q_scale = sb.tile([P, Q], U8, name="q_scale", align_bytes=64)
        nc.vector.quantize_mx(out=q_codes[:].bitcast(FP8X4), scales=q_scale[:], in_=q_bf[:].rearrange("p q j -> p (q j)"))

        v_raw0 = sb.tile([P, PACK, E], F32, name="v_raw0", align_bytes=64)
        nc.sync.dma_start(out=v_raw0[:], in_=vals[0:K_PASS, :].rearrange("(p j) e -> p j e", j=PACK))
        v_raw = {(0, h): v_raw0[:, :, h * OUT_N : (h + 1) * OUT_N] for h in range(2)}

        scores = sb.tile([P, T], F32, name="scores")
        score_bank = []
        start = 0
        for n, width in enumerate(SCORE_WIDTHS):
            cols = slice(start, start + width)
            start = start + width
            bank = ps.tile([P, width], F32, name=f"score_bank{n}", tag=f"bank{n}")
            nc.tensor.matmul_mx(
                out=bank[:],
                lhsT=q_codes[:].bitcast(FP8X4),
                lhsT_scale=q_scale[:],
                rhs=key_words[:, 2 * cols.start : 2 * cols.stop].bitcast(FP4X4),
                rhs_scale=key_scale[:, cols],
                start=True,
                stop=True,
            )
            score_bank.append(bank)
            if n in (0, 2):
                nc.scalar.activation(scores[:, cols], bank[:], ACT.Copy)
            else:
                nc.vector.tensor_copy(out=scores[:, cols], in_=bank[:])

        for h in range(2):
            raw = sb.tile([P, PACK, OUT_N], F32, name=f"v_raw1{h}", tag=f"stage{2 + h}", align_bytes=64)
            nc.sync.dma_start(
                out=raw[:], in_=vals[K_PASS:T, h * OUT_N : (h + 1) * OUT_N].rearrange("(p j) e -> p j e", j=PACK)
            )
            v_raw[(1, h)] = raw[:]

        fac_cols = sb.tile([P, PASSES, PACK], F32, name="fac_cols")
        nc.sync.dma_start(out=fac_cols[:], in_=fac.rearrange("o (g p j) -> p (o g) j", g=PASSES, j=PACK))

        fac_bank = []
        for g in range(PASSES):
            bank = ps.tile([P, PACK, P], F32, name=f"fac_bank{g}")
            for j in range(PACK):
                nc.tensor.transpose(bank[:, j, :], fac_cols[:, g, j : j + 1].to_broadcast([P, P]), ident[:])
            fac_bank.append(bank)

        first, second = slice(0, LIST_COLS), slice(LIST_COLS, 2 * LIST_COLS)
        own_a = sb.tile([P, HALF], F32, name="own_a")
        nc.vector.tensor_copy(out=own_a[:], in_=scores[:].indirect(list1[:, first]))
        other_a = sb.tile([P, HALF], F32, name="other_a")
        nc.scalar.activation(other_a[:], scores[:].indirect(list2[:, first]), ACT.Copy)
        own_b = sb.tile([P, HALF], F32, name="own_b", tag="hold0", align_bytes=64)
        nc.scalar.activation(own_b[:], scores[:].indirect(list1[:, second]), ACT.Copy)
        other_b = sb.tile([P, HALF], F32, name="other_b", tag="hold1", align_bytes=64)
        nc.scalar.activation(other_b[:], scores[:].indirect(list2[:, second]), ACT.Copy)
        gap_a = sb.tile([P, HALF], F32, name="gap_a")
        nc.vector.tensor_tensor(out=gap_a[:], in0=other_a[:], in1=own_a[:], op=ALU.subtract)
        nc.vector.tensor_tensor(out=moved[:].indirect(list1[:, first]), in0=gap_a[:], in1=share_wide[:], op=ALU.mult)
        own_bs = sb.tile([P, HALF], F32, name="own_bs")
        nc.scalar.activation(own_bs[:], own_b[:], ACT.Copy, scale=share_neg[:])
        other_bs = sb.tile([P, HALF], F32, name="other_bs")
        nc.scalar.activation(other_bs[:], other_b[:], ACT.Copy, scale=share_col[:])
        nc.vector.tensor_tensor(out=moved[:].indirect(list1[:, second]), in0=other_bs[:], in1=own_bs[:], op=ALU.add)

        v_bf, v_codes, v_scale = {}, {}, {}

        def round_values(g, h, tag):
            v_bf[(g, h)] = sb.tile([P, OUT_N, PACK], BF16, name=f"v_bf{g}{h}", tag=tag, align_bytes=64)
            nc.scalar.copy(
                out=v_bf[(g, h)][:].rearrange("p (c i) j -> p c j i", i=4),
                in_=v_raw[(g, h)].rearrange("p j (c i) -> p c j i", i=4),
            )

        def quantise_values(g, h):
            v_codes[(g, h)] = sb.tile([P, OUT_N], U32, name=f"v_codes{g}{h}", align_bytes=64)
            v_scale[(g, h)] = sb.tile([P, OUT_N], U8, name=f"v_scale{g}{h}", align_bytes=64)
            nc.vector.quantize_mx(
                out=v_codes[(g, h)][:].bitcast(FP8X4),
                scales=v_scale[(g, h)][:],
                in_=v_bf[(g, h)][:].rearrange("p e j -> p (e j)"),
            )

        round_values(0, 0, "hold0")
        round_values(0, 1, "hold1")
        round_values(1, 0, "hold2")

        s = sb.tile([P, T], F32, name="s", tag="hold3", align_bytes=64)
        for n in range(3):
            cols = slice(n * 256, (n + 1) * 256)
            nc.vector.tensor_tensor(out=s[:, cols], in0=score_bank[n][:], in1=moved[:, cols], op=ALU.add)
        nc.gpsimd.tensor_tensor(out=s[:, 768:T], in0=scores[:, 768:T], in1=moved[:, 768:T], op=ALU.add)
        neg_max = sb.tile([P, 1], F32, name="neg_max")
        nc.vector.tensor_reduce(out=neg_max[:], in_=s[:], axis=AXIS.X, op=ALU.max, negate=True)
        p = sb.tile([P, T], F32, name="p", tag="stage2", align_bytes=64)
        row_sum = sb.tile([P, 1], F32, name="row_sum")
        nc.scalar.activation(p[:], s[:], ACT.Exp, bias=neg_max[:], accum_out=row_sum[:])
        round_values(1, 1, "hold3")
        quantise_values(0, 0)
        quantise_values(0, 1)
        quantise_values(1, 0)
        inv_sum = sb.tile([P, 1], F32, name="inv_sum")
        nc.vector.reciprocal(out=inv_sum[:], in_=row_sum[:])

        early = sb.tile([P, K_PASS // 2], F32, name="early")
        nc.vector.tensor_tensor(
            out=early[:].rearrange("q (p e) -> q p e", e=2),
            in0=p[:, K_PASS:T].rearrange("q (p j) -> q p j", j=PACK)[:, :, 2:4],
            in1=fac_bank[1][:, 2:4, :].rearrange("q e p -> q p e"),
            op=ALU.mult,
        )

        out_parts = ((0, 0, 256), (1, 0, 128), (1, 128, 128))
        out_bank = [
            ps.tile([P, width], F32, name=f"out_bank{n}", tag=f"bank{2 + n}") for n, (h, first_col, width) in enumerate(out_parts)
        ]
        w_turned = []
        for g in range(PASSES):
            turn_bank = ps.tile([P, 2, Q], F32, name=f"turn_bank{g}", tag=f"bank{g}")
            p_pass = p[:, g * K_PASS : (g + 1) * K_PASS].rearrange("q (p j) -> q p j", j=PACK)
            for u in range(2):
                w_bf = sb.tile([P, K_PASS // 2], BF16, name=f"w_bf{g}{u}", align_bytes=64)
                if (g, u) == (1, 1):
                    nc.vector.tensor_scalar(out=w_bf[:], in0=early[:], scalar1=inv_sum[:], scalar2=None, op0=ALU.mult)
                else:
                    nc.vector.scalar_tensor_tensor(
                        out=w_bf[:].rearrange("q (p e) -> q p e", e=2),
                        in0=p_pass[:, :, 2 * u : 2 * u + 2],
                        scalar=inv_sum[:],
                        in1=fac_bank[g][:, 2 * u : 2 * u + 2, :].rearrange("q e p -> q p e"),
                        op0=ALU.mult,
                        op1=ALU.mult,
                    )
                nc.tensor.transpose(turn_bank[:, u, :], w_bf[:].bitcast(F32), ident[:])
            wt_bf = sb.tile([P, Q * PACK], BF16, name=f"wt_bf{g}", align_bytes=64)
            nc.scalar.copy(
                out=wt_bf[:].bitcast(F32).rearrange("p (q u) -> p q u", u=2),
                in_=turn_bank[:].rearrange("p u q -> p q u"),
            )
            w_turned.append(wt_bf)
        quantise_values(1, 1)
        for g in range(PASSES):
            w_codes = sb.tile([P, Q], U32, name=f"w_codes{g}", align_bytes=64)
            w_scale = sb.tile([P, Q], U8, name=f"w_scale{g}", align_bytes=64)
            nc.vector.quantize_mx(out=w_codes[:].bitcast(FP8X4), scales=w_scale[:], in_=w_turned[g][:])
            for n, (h, first_col, width) in enumerate(out_parts):
                cols = slice(first_col, first_col + width)
                nc.tensor.matmul_mx(
                    out=out_bank[n][:],
                    lhsT=w_codes[:].bitcast(FP8X4),
                    lhsT_scale=w_scale[:],
                    rhs=v_codes[(g, h)][:, cols].bitcast(FP8X4),
                    rhs_scale=v_scale[(g, h)][:, cols],
                    start=(g == 0),
                    stop=(g == PASSES - 1),
                )
        for h in range(E // OUT_N):
            cols = slice(h * OUT_N, (h + 1) * OUT_N)
            res = sb.tile([P, OUT_N], F32, name=f"res{h}")
            if h == 0:
                nc.vector.tensor_copy(out=res[:], in_=out_bank[0][:])
                nc.sync.dma_start(out=out[:, cols], in_=res[:])
            else:
                nc.scalar.copy(out=res[:, 0:128], in_=out_bank[1][:])
                nc.scalar.copy(out=res[:, 128:256], in_=out_bank[2][:])
                nc.scalar.dma_start(out=out[:, cols], in_=res[:])
